import numpy as np
import ml_dtypes


def mxq(x, axis, fmt="e4m3"):
    dtype, down = {"e4m3": (ml_dtypes.float8_e4m3fn, 7), "e5m2": (ml_dtypes.float8_e5m2, 14)}[fmt]
    v = np.moveaxis(np.asarray(x, np.float32).astype(ml_dtypes.bfloat16).astype(np.float64), axis, -1)
    blocks = v.reshape(v.shape[:-1] + (-1, 32))
    amax = np.abs(blocks).max(-1, keepdims=True)
    byte = np.maximum(np.where(amax > 0, np.frexp(amax)[1] - 1 + 127, 0) - down, 1)
    scale = np.exp2(byte - 127.0)
    codes = (blocks / scale).astype(np.float32).astype(dtype).astype(np.float64)
    return np.moveaxis((codes * scale).reshape(v.shape), -1, axis)


WIDE = False


def mx_kscale(k):
    if not WIDE:
        return np.ones(k)
    levels = np.array([10, -10, 5, -5, 0])
    if k % 512:
        return np.exp2(np.random.permutation(np.resize(levels, k // 32))).repeat(32)
    a = np.empty((k // 512, 16))
    for p in range(k // 512):
        a[p, :8] = np.random.permutation(np.resize(levels, 8))
        for g in range(8):
            far = levels[np.abs(levels - a[p, g]) >= 10]
            a[p, g + 8] = far[np.random.randint(len(far))]
    return np.exp2(a.ravel()).repeat(32)


def f64(x):
    return np.asarray(x).astype(np.float64)


def striped(idx):
    return np.tile(idx.reshape(-1, 16).T, (8, 1)).astype(np.uint16)


def unstriped(offs):
    return offs[:16].T.reshape(-1).astype(np.int64)


K, T, D, S, V, H, N = 512, 2048, 2, 1024, 512, 1024, 128
P = 2 ** 7


def setup_inputs():
    n = np.random.standard_normal
    s = mx_kscale(K)[:, None]
    u = mx_kscale(H)
    q = np.random.permutation(S)
    return {
        "xT": (n((K, T)) * s).astype(np.float32),
        "w1": (n((K, H)) / np.sqrt(K) / s * u).astype(np.float32),
        "w2": (n((H, N)) / np.sqrt(H) / u[:, None]).astype(np.float32),
        "gate": np.tile(np.random.uniform(0.2, 1.0, (D, 1, V)) / np.sqrt(D), (1, P, 1)).astype(np.float32),
        "offs": striped(np.random.permutation(T)[:S]),
        "pos1": striped(q[:V]),
        "pos2": striped(q[V:]),
    }


def reference(xT, w1, w2, gate, offs, pos1, pos2):
    h = mxq(f64(w1), 0, "e4m3").T @ mxq(f64(xT)[:, unstriped(offs)], 0, "e4m3")
    z = sum(f64(gate)[d, :1] * h[:, unstriped(p)] for d, p in enumerate((pos1, pos2)))
    return mxq(f64(w2), 0, "e4m3").T @ mxq(z, 0, "e4m3")

@@ -1,0 +1,262 @@
+from contextlib import ExitStack
+
+import concourse.mybir as mybir
+
+K, T, S, V, H, N = 512, 2048, 1024, 512, 1024, 128
+P = 128
+FLOPS = 2 * K * H * S + 2 * H * N * V
+
+F32 = mybir.dt.float32
+BF16 = mybir.dt.bfloat16
+U32 = mybir.dt.uint32
+U16 = mybir.dt.uint16
+U8 = mybir.dt.uint8
+FP8X4 = mybir.dt.float8_e4m3fn_x4
+COPY = mybir.ActivationFunctionType.Copy
+MULT = mybir.AluOpType.mult
+ADD = mybir.AluOpType.add
+
+
+def tile_picked_sage_none_e_kernel(tc, xT, w1, w2, gate, offs, pos1, pos2, out):
+    nc = tc.nc
+    with ExitStack() as ctx:
+        lists = ctx.enter_context(tc.tile_pool(name="lists", bufs=1))
+        sb = ctx.enter_context(tc.tile_pool(name="sb", bufs=1))
+        ps = ctx.enter_context(tc.psum_pool(name="ps", bufs=6))
+        pso = ctx.enter_context(tc.psum_pool(name="pso", bufs=2))
+
+        offs_t = lists.tile([P, S // 16], U16, name="offs_t")
+        pos1_t = lists.tile([P, V // 16], U16, name="pos1_t")
+        pos2_t = lists.tile([P, V // 16], U16, name="pos2_t")
+
+        warm = sb.tile([P, 1], F32, name="warm")
+        warm_out = sb.tile([P, 1], F32, name="warm_out")
+        nc.gpsimd.memset(warm[:], 0.0)
+        nc.scalar.activation(warm_out[:], warm[:], COPY)
+
+        x_view = xT.rearrange("(p j) t -> p j t", j=4)
+        x_raw = []
+        for u, c0, c1 in ((0, 0, 1024), (0, 1024, 2048), (1, 0, 1024), (1, 1024, 1536), (1, 1536, 1792), (1, 1792, 2048)):
+            raw = sb.tile([P, 2, c1 - c0], F32, name="x_raw_%d_%d" % (u, c0))
+            nc.sync.dma_start(raw[:], x_view[:, 2 * u : 2 * u + 2, c0:c1])
+            x_raw.append((u, c0, raw))
+            if len(x_raw) == 1:
+                nc.sync.dma_start(offs_t[:], offs)
+        w1_view = w1.rearrange("(p j) i -> p j i", j=4)
+        w1_raw = []
+
+        def load_w1(piece):
+            raw = sb.tile([P, 4, 256], F32, name="w1_raw_%d" % piece)
+            nc.sync.dma_start(raw[:], w1_view[:, :, 256 * piece : 256 * piece + 256])
+            w1_raw.append(raw)
+
+        load_w1(0)
+        load_w1(1)
+        w2_raw = sb.tile([P, 2, 4, N], F32, name="w2_raw")
+        w2_view = w2.rearrange("(g p t) n -> g p t n", g=2, t=4)
+        for g in range(2):
+            nc.sync.dma_start(w2_raw[:, g], w2_view[g])
+        nc.sync.dma_start(pos1_t[:], pos1)
+        nc.sync.dma_start(pos2_t[:], pos2)
+        gates = sb.tile([P, 2, V], F32, name="gates")
+        nc.sync.dma_start(gates[:], gate.rearrange("d p v -> p d v"))
+        load_w1(2)
+        load_w1(3)
+
+        pairs = []
+        for u in range(2):
+            pt = sb.tile([P, T, 2], BF16, name="pairs_%d" % u)
+            pairs.append(pt)
+        picked = sb.tile([P, S, 4], BF16, name="picked", align_bytes=64)
+        picked_words = picked[:].rearrange("p n q -> p (n q)").bitcast(U32).rearrange("p (n u) -> p n u", u=2)
+        xc = sb.tile([P, S], U32, name="xc", align_bytes=64)
+        xs = sb.tile([P, S], U8, name="xs", align_bytes=64)
+
+        def cast_x(i, a, b, scalar):
+            u, c0, raw = x_raw[i]
+            dst = pairs[u][:, c0 + a : c0 + b, :]
+            src = raw[:, :, a:b].rearrange("p e t -> p t e")
+            if scalar:
+                nc.scalar.activation(dst, src, COPY)
+            else:
+                nc.vector.tensor_copy(dst, src)
+
+        def gather_x(u, n0, n1):
+            window = pairs[u][:].rearrange("p t e -> p (t e)").bitcast(U32)
+            nc.vector.tensor_copy(picked_words[:, n0:n1, u], window.indirect(offs_t[:, n0 // 16 : n1 // 16]))
+
+        def quant_x(n0, n1):
+            nc.vector.quantize_mx(
+                out=xc[:, n0:n1].bitcast(FP8X4),
+                scales=xs[:, n0:n1],
+                in_=picked[:, n0:n1, :].rearrange("p n q -> p (n q)"),
+            )
+
+        w1b, w1c, w1s = [], [], []
+        for g in range(2):
+            b = sb.tile([P, 4, P, 4], BF16, name="w1b_%d" % g, align_bytes=64)
+            c = sb.tile([P, 4 * P], U32, name="w1c_%d" % g, align_bytes=64)
+            s = sb.tile([P, 4 * P], U8, name="w1s_%d" % g, align_bytes=64)
+            w1b.append(b)
+            w1c.append(c)
+            w1s.append(s)
+
+        def cast_w1(piece, t0, t1):
+            g, half = divmod(piece, 2)
+            dst = w1b[g][:, t0:t1, 64 * half : 64 * half + 64, :].rearrange("p t m j -> p m t j")
+            src = w1_raw[piece][:].rearrange("p j (m t) -> p m t j", t=4)[:, :, t0:t1, :]
+            nc.scalar.activation(dst, src, COPY)
+
+        def quant_w1(g, t0, t1):
+            nc.vector.quantize_mx(
+                out=w1c[g][:, P * t0 : P * t1].bitcast(FP8X4),
+                scales=w1s[g][:, P * t0 : P * t1],
+                in_=w1b[g][:, t0:t1].rearrange("p t m j -> p (t m j)"),
+            )
+
+        w2b = sb.tile([P, 2, N, 4], BF16, name="w2b", align_bytes=64)
+        w2c = sb.tile([P, 2 * N], U32, name="w2c", align_bytes=64)
+        w2s = sb.tile([P, 2 * N], U8, name="w2s", align_bytes=64)
+
+        h = []
+        for b in range(8):
+            ht = sb.tile([P, S], F32, name="h_%d" % b)
+            h.append(ht)
+        t01, z, zc, zs = [], [], [], []
+        for g in range(2):
+            pair = []
+            for d in range(2):
+                tt = sb.tile([P, 4, V], F32, name="term_%d_%d" % (g, d))
+                pair.append(tt)
+            t01.append(pair)
+            zt = sb.tile([P, V, 4], BF16, name="z_%d" % g, align_bytes=64)
+            zct = sb.tile([P, V], U32, name="zc_%d" % g, align_bytes=64)
+            zst = sb.tile([P, V], U8, name="zs_%d" % g, align_bytes=64)
+            z.append(zt)
+            zc.append(zct)
+            zs.append(zst)
+        out_t = sb.tile([P, V], F32, name="out_t")
+
+        def layer1(b):
+            g, t = divmod(b, 4)
+            for half in range(2):
+                n = slice(512 * half, 512 * half + 512)
+                acc = ps.tile([P, 512], F32, name="acc")
+                nc.tensor.matmul_mx(
+                    out=acc[:],
+                    lhsT=w1c[g][:, P * t : P * t + P].bitcast(FP8X4),
+                    lhsT_scale=w1s[g][:, P * t : P * t + P],
+                    rhs=xc[:, n].bitcast(FP8X4),
+                    rhs_scale=xs[:, n],
+                    start=True,
+                    stop=True,
+                )
+                nc.scalar.activation(h[b][:, n], acc[:], COPY)
+
+        pos = (pos1_t, pos2_t)
+
+        def gather_h(b, d, v0, v1):
+            g, t = divmod(b, 4)
+            nc.vector.tensor_tensor(
+                t01[g][d][:, t, v0:v1],
+                h[b][:].indirect(pos[d][:, v0 // 16 : v1 // 16]),
+                gates[:, d, v0:v1],
+                MULT,
+            )
+
+        def add_z(g, v0, v1):
+            dst = z[g][:, v0:v1, :].rearrange("p (c i) t -> p c t i", i=4)
+            a = t01[g][0][:, :, v0:v1].rearrange("p t (c i) -> p c t i", i=4)
+            b = t01[g][1][:, :, v0:v1].rearrange("p t (c i) -> p c t i", i=4)
+            nc.vector.tensor_tensor(dst, a, b, ADD)
+
+        def quant_z(g, v0, v1):
+            nc.vector.quantize_mx(
+                out=zc[g][:, v0:v1].bitcast(FP8X4),
+                scales=zs[g][:, v0:v1],
+                in_=z[g][:, v0:v1, :].rearrange("p v t -> p (v t)"),
+            )
+
+        def layer2(v0, v1):
+            acc = pso.tile([P, v1 - v0], F32, name="acc_out")
+            for g in range(2):
+                nc.tensor.matmul_mx(
+                    out=acc[:],
+                    lhsT=w2c[:, N * g : N * g + N].bitcast(FP8X4),
+                    lhsT_scale=w2s[:, N * g : N * g + N],
+                    rhs=zc[g][:, v0:v1].bitcast(FP8X4),
+                    rhs_scale=zs[g][:, v0:v1],
+                    start=g == 0,
+                    stop=g == 1,
+                )
+            nc.scalar.activation(out_t[:, v0:v1], acc[:], COPY)
+            nc.sync.dma_start(out[:, v0:v1], out_t[:, v0:v1])
+
+        cast_x(0, 0, 512, False)
+        cast_x(0, 512, 1024, True)
+        cast_x(1, 0, 704, False)
+        cast_x(1, 704, 1024, True)
+        gather_x(0, 0, 1024)
+        cast_x(2, 0, 640, True)
+        cast_x(2, 640, 1024, False)
+        cast_x(3, 0, 512, False)
+        cast_x(4, 0, 256, True)
+        cast_x(5, 0, 256, False)
+        gather_x(1, 0, 512)
+        gather_x(1, 512, 1024)
+        cast_w1(0, 0, 4)
+        cast_w1(1, 0, 1)
+        cast_w1(1, 1, 4)
+        quant_x(0, 512)
+        quant_w1(0, 0, 1)
+        quant_x(512, 1024)
+        layer1(0)
+        quant_w1(0, 1, 2)
+        quant_w1(0, 2, 4)
+        layer1(1)
+        nc.vector.tensor_copy(w2b[:], w2_raw[:].rearrange("p g t n -> p g n t"))
+        layer1(2)
+        layer1(3)
+        gather_h(0, 0, 0, V)
+        gather_h(0, 1, 0, V)
+        nc.vector.quantize_mx(
+            out=w2c[:].bitcast(FP8X4), scales=w2s[:], in_=w2b[:].rearrange("p g n t -> p (g n t)")
+        )
+        gather_h(1, 0, 0, V)
+        gather_h(1, 1, 0, V)
+        cast_w1(2, 0, 2)
+        cast_w1(2, 2, 4)
+        gather_h(2, 0, 0, V)
+        gather_h(2, 1, 0, V)
+        cast_w1(3, 0, 2)
+        cast_w1(3, 2, 4)
+        gather_h(3, 0, 0, V)
+        quant_w1(1, 0, 4)
+        gather_h(3, 1, 0, V)
+        layer1(4)
+        layer1(5)
+        gather_h(4, 0, 0, V)
+        add_z(0, 0, 256)
+        gather_h(4, 1, 0, V)
+        quant_z(0, 0, 256)
+        add_z(0, 256, 512)
+        layer1(6)
+        gather_h(5, 0, 0, V)
+        quant_z(0, 256, 512)
+        gather_h(5, 1, 0, V)
+        layer1(7)
+        gather_h(6, 0, 0, V)
+        gather_h(6, 1, 0, V)
+        gather_h(7, 0, 0, 256)
+        gather_h(7, 1, 0, 256)
+        gather_h(7, 0, 256, 512)
+        add_z(1, 0, 256)
+        gather_h(7, 1, 256, 512)
+        quant_z(1, 0, 256)
+        layer2(0, 256)
+        add_z(1, 256, 384)
+        add_z(1, 384, 512)
+        quant_z(1, 256, 384)
+        layer2(256, 384)
+        quant_z(1, 384, 512)
+        layer2(384, 512)

@@ -1,6 +1,7 @@
 from contextlib import ExitStack
 
 import concourse.mybir as mybir
+from concourse.masks import make_identity
 
 K, T, S, V, H, N = 512, 2048, 1024, 512, 1024, 128
 P = 128
@@ -22,8 +23,10 @@ def tile_picked_sage_none_e_kernel(tc, xT, w1, w2, gate, offs, pos1, pos2, out):
     with ExitStack() as ctx:
         lists = ctx.enter_context(tc.tile_pool(name="lists", bufs=1))
         sb = ctx.enter_context(tc.tile_pool(name="sb", bufs=1))
-        ps = ctx.enter_context(tc.psum_pool(name="ps", bufs=6))
-        pso = ctx.enter_context(tc.psum_pool(name="pso", bufs=2))
+        ps = ctx.enter_context(tc.psum_pool(name="ps", bufs=1))
+        ps_o = ctx.enter_context(tc.psum_pool(name="ps_o", bufs=3))
+        ps_t = ctx.enter_context(tc.psum_pool(name="ps_t", bufs=2))
+        ps_b = ctx.enter_context(tc.psum_pool(name="ps_b", bufs=2))
 
         offs_t = lists.tile([P, S // 16], U16, name="offs_t")
         pos1_t = lists.tile([P, V // 16], U16, name="pos1_t")
@@ -33,10 +36,14 @@ def tile_picked_sage_none_e_kernel(tc, xT, w1, w2, gate, offs, pos1, pos2, out):
         warm_out = sb.tile([P, 1], F32, name="warm_out")
         nc.gpsimd.memset(warm[:], 0.0)
         nc.scalar.activation(warm_out[:], warm[:], COPY)
+        ident32 = sb.tile([P, P], F32, name="ident32")
+        ident16 = sb.tile([P, P], BF16, name="ident16")
+        make_identity(nc, ident32[:])
+        make_identity(nc, ident16[:])
 
         x_view = xT.rearrange("(p j) t -> p j t", j=4)
         x_raw = []
-        for u, c0, c1 in ((0, 0, 1024), (0, 1024, 2048), (1, 0, 1024), (1, 1024, 1536), (1, 1536, 1792), (1, 1792, 2048)):
+        for u, c0, c1 in ((0, 0, 1024), (0, 1024, 1536), (0, 1536, 2048), (1, 0, 1024), (1, 1024, 1536), (1, 1536, 1792), (1, 1792, 2048)):
             raw = sb.tile([P, 2, c1 - c0], F32, name="x_raw_%d_%d" % (u, c0))
             nc.sync.dma_start(raw[:], x_view[:, 2 * u : 2 * u + 2, c0:c1])
             x_raw.append((u, c0, raw))
@@ -69,7 +76,7 @@ def tile_picked_sage_none_e_kernel(tc, xT, w1, w2, gate, offs, pos1, pos2, out):
             pairs.append(pt)
         picked = sb.tile([P, S, 4], BF16, name="picked", align_bytes=64)
         picked_words = picked[:].rearrange("p n q -> p (n q)").bitcast(U32).rearrange("p (n u) -> p n u", u=2)
-        xc = sb.tile([P, S], U32, name="xc", align_bytes=64)
+        xc0 = sb.tile([P, 512], U32, name="xc0", align_bytes=64)
         xs = sb.tile([P, S], U8, name="xs", align_bytes=64)
 
         def cast_x(i, a, b, scalar):
@@ -87,23 +94,28 @@ def tile_picked_sage_none_e_kernel(tc, xT, w1, w2, gate, offs, pos1, pos2, out):
 
         def quant_x(n0, n1):
             nc.vector.quantize_mx(
-                out=xc[:, n0:n1].bitcast(FP8X4),
+                out=xc[n0 // 512][:].bitcast(FP8X4),
                 scales=xs[:, n0:n1],
                 in_=picked[:, n0:n1, :].rearrange("p n q -> p (n q)"),
             )
 
         w1b, w1c, w1s = [], [], []
         for g in range(2):
-            b = sb.tile([P, 4, P, 4], BF16, name="w1b_%d" % g, align_bytes=64)
+            b = [None, None]
+            b[0] = sb.tile([P, 1, P, 4], BF16, name="w1b_%d_0" % g, align_bytes=64)
+            b[1] = sb.tile([P, 3, P, 4], BF16, name="w1b_%d_1" % g, align_bytes=64)
             c = sb.tile([P, 4 * P], U32, name="w1c_%d" % g, align_bytes=64)
             s = sb.tile([P, 4 * P], U8, name="w1s_%d" % g, align_bytes=64)
             w1b.append(b)
             w1c.append(c)
             w1s.append(s)
+        xc1 = sb.tile([P, 512], U32, name="xc1", tag="w1b_0_0", align_bytes=64)
+        xc = (xc0, xc1)
 
-        def cast_w1(piece, t0, t1):
+        def cast_w1(piece, rest):
             g, half = divmod(piece, 2)
-            dst = w1b[g][:, t0:t1, 64 * half : 64 * half + 64, :].rearrange("p t m j -> p m t j")
+            t0, t1 = ((0, 1), (1, 4))[rest]
+            dst = w1b[g][rest][:, :, 64 * half : 64 * half + 64, :].rearrange("p t m j -> p m t j")
             src = w1_raw[piece][:].rearrange("p j (m t) -> p m t j", t=4)[:, :, t0:t1, :]
             nc.scalar.activation(dst, src, COPY)
 
@@ -111,10 +123,10 @@ def tile_picked_sage_none_e_kernel(tc, xT, w1, w2, gate, offs, pos1, pos2, out):
             nc.vector.quantize_mx(
                 out=w1c[g][:, P * t0 : P * t1].bitcast(FP8X4),
                 scales=w1s[g][:, P * t0 : P * t1],
-                in_=w1b[g][:, t0:t1].rearrange("p t m j -> p (t m j)"),
+                in_=w1b[g][min(t0, 1)][:, max(t0 - 1, 0) : max(t1 - 1, 1)].rearrange("p t m j -> p (t m j)"),
             )
 
-        w2b = sb.tile([P, 2, N, 4], BF16, name="w2b", align_bytes=64)
+        w2b = sb.tile([P, 2, N, 4], BF16, name="w2b", tag="w1b_0_1", align_bytes=64)
         w2c = sb.tile([P, 2 * N], U32, name="w2c", align_bytes=64)
         w2s = sb.tile([P, 2 * N], U8, name="w2s", align_bytes=64)
 
@@ -126,8 +138,16 @@ def tile_picked_sage_none_e_kernel(tc, xT, w1, w2, gate, offs, pos1, pos2, out):
         for g in range(2):
             pair = []
             for d in range(2):
-                tt = sb.tile([P, 4, V], F32, name="term_%d_%d" % (g, d))
-                pair.append(tt)
+                if g:
+                    tt = sb.tile([P, 4, V], F32, name="term_%d" % d)
+                    pair.append([tt[:, t] for t in range(4)] + [tt])
+                else:
+                    blocks = []
+                    for t in range(4):
+                        tag = "w1b_1_%d" % d if t == 3 else "term_%d_%d" % (t, d)
+                        tt = sb.tile([P, V], F32, name="term_%d_%d" % (t, d), tag=tag, align_bytes=64)
+                        blocks.append(tt)
+                    pair.append(blocks)
             t01.append(pair)
             zt = sb.tile([P, V, 4], BF16, name="z_%d" % g, align_bytes=64)
             zct = sb.tile([P, V], U32, name="zc_%d" % g, align_bytes=64)
@@ -141,12 +161,12 @@ def tile_picked_sage_none_e_kernel(tc, xT, w1, w2, gate, offs, pos1, pos2, out):
             g, t = divmod(b, 4)
             for half in range(2):
                 n = slice(512 * half, 512 * half + 512)
-                acc = ps.tile([P, 512], F32, name="acc")
+                acc = (ps_o if half else ps).tile([P, 512], F32, name="acc_%d" % half)
                 nc.tensor.matmul_mx(
                     out=acc[:],
                     lhsT=w1c[g][:, P * t : P * t + P].bitcast(FP8X4),
                     lhsT_scale=w1s[g][:, P * t : P * t + P],
-                    rhs=xc[:, n].bitcast(FP8X4),
+                    rhs=xc[half][:].bitcast(FP8X4),
                     rhs_scale=xs[:, n],
                     start=True,
                     stop=True,
@@ -158,7 +178,7 @@ def tile_picked_sage_none_e_kernel(tc, xT, w1, w2, gate, offs, pos1, pos2, out):
         def gather_h(b, d, v0, v1):
             g, t = divmod(b, 4)
             nc.vector.tensor_tensor(
-                t01[g][d][:, t, v0:v1],
+                t01[g][d][t][:, v0:v1],
                 h[b][:].indirect(pos[d][:, v0 // 16 : v1 // 16]),
                 gates[:, d, v0:v1],
                 MULT,
@@ -166,9 +186,35 @@ def tile_picked_sage_none_e_kernel(tc, xT, w1, w2, gate, offs, pos1, pos2, out):
 
         def add_z(g, v0, v1):
             dst = z[g][:, v0:v1, :].rearrange("p (c i) t -> p c t i", i=4)
-            a = t01[g][0][:, :, v0:v1].rearrange("p t (c i) -> p c t i", i=4)
-            b = t01[g][1][:, :, v0:v1].rearrange("p t (c i) -> p c t i", i=4)
+            a = t01[g][0][4][:, :, v0:v1].rearrange("p t (c i) -> p c t i", i=4)
+            b = t01[g][1][4][:, :, v0:v1].rearrange("p t (c i) -> p c t i", i=4)
             nc.vector.tensor_tensor(dst, a, b, ADD)
+
+        back = {}
+
+        def fold(b, v0, v1):
+            g, t = divmod(b, 4)
+            sum_t = ps_t.tile([P, v1 - v0], F32, name="sum_t")
+            for v in range(v0, v1, P):
+                for d in range(2):
+                    nc.tensor.matmul(
+                        out=sum_t[:, v - v0 : v - v0 + P],
+                        lhsT=t01[g][d][t][:, v : v + P],
+                        rhs=ident32[:],
+                        start=d == 0,
+                        stop=d == 1,
+                        is_transpose=True,
+                    )
+            z_t = sb.tile([P, v1 - v0], BF16, name="z_t_%d" % b)
+            nc.scalar.activation(z_t[:], sum_t[:], COPY)
+            for v in range(v0, v1, P):
+                key = (g, v // 256)
+                if key not in back:
+                    back[key] = ps_b.tile([P, 4, 256], BF16, name="back")
+                nc.tensor.transpose(back[key][:, t, v % 256 : v % 256 + P], z_t[:, v - v0 : v - v0 + P], ident16[:])
+
+        def weave_z(g, half):
+            nc.scalar.copy(z[g][:, 256 * half : 256 * half + 256, :], back[g, half][:].rearrange("p t v -> p v t"))
 
         def quant_z(g, v0, v1):
             nc.vector.quantize_mx(
@@ -178,7 +224,7 @@ def tile_picked_sage_none_e_kernel(tc, xT, w1, w2, gate, offs, pos1, pos2, out):
             )
 
         def layer2(v0, v1):
-            acc = pso.tile([P, v1 - v0], F32, name="acc_out")
+            acc = ps_o.tile([P, v1 - v0], F32, name="acc_1")
             for g in range(2):
                 nc.tensor.matmul_mx(
                     out=acc[:],
@@ -194,19 +240,21 @@ def tile_picked_sage_none_e_kernel(tc, xT, w1, w2, gate, offs, pos1, pos2, out):
 
         cast_x(0, 0, 512, False)
         cast_x(0, 512, 1024, True)
-        cast_x(1, 0, 704, False)
-        cast_x(1, 704, 1024, True)
+        cast_x(1, 0, 512, False)
+        cast_x(2, 0, 352, False)
+        cast_x(2, 352, 512, True)
         gather_x(0, 0, 1024)
-        cast_x(2, 0, 640, True)
-        cast_x(2, 640, 1024, False)
-        cast_x(3, 0, 512, False)
-        cast_x(4, 0, 256, True)
-        cast_x(5, 0, 256, False)
+        cast_x(3, 0, 704, True)
+        cast_x(3, 704, 1024, False)
+        cast_x(4, 0, 512, False)
+        cast_x(5, 0, 256, True)
+        cast_x(6, 0, 256, False)
         gather_x(1, 0, 512)
         gather_x(1, 512, 1024)
-        cast_w1(0, 0, 4)
-        cast_w1(1, 0, 1)
-        cast_w1(1, 1, 4)
+        cast_w1(0, 0)
+        cast_w1(0, 1)
+        cast_w1(1, 0)
+        cast_w1(1, 1)
         quant_x(0, 512)
         quant_w1(0, 0, 1)
         quant_x(512, 1024)
@@ -217,6 +265,10 @@ def tile_picked_sage_none_e_kernel(tc, xT, w1, w2, gate, offs, pos1, pos2, out):
         nc.vector.tensor_copy(w2b[:], w2_raw[:].rearrange("p g t n -> p g n t"))
         layer1(2)
         layer1(3)
+        cast_w1(2, 0)
+        cast_w1(3, 0)
+        cast_w1(2, 1)
+        cast_w1(3, 1)
         gather_h(0, 0, 0, V)
         gather_h(0, 1, 0, V)
         nc.vector.quantize_mx(
@@ -224,38 +276,45 @@ def tile_picked_sage_none_e_kernel(tc, xT, w1, w2, gate, offs, pos1, pos2, out):
         )
         gather_h(1, 0, 0, V)
         gather_h(1, 1, 0, V)
-        cast_w1(2, 0, 2)
-        cast_w1(2, 2, 4)
+        fold(0, 0, V)
         gather_h(2, 0, 0, V)
         gather_h(2, 1, 0, V)
-        cast_w1(3, 0, 2)
-        cast_w1(3, 2, 4)
-        gather_h(3, 0, 0, V)
-        quant_w1(1, 0, 4)
-        gather_h(3, 1, 0, V)
+        quant_w1(1, 0, 1)
         layer1(4)
+        fold(1, 0, V)
+        gather_h(3, 0, 0, V)
+        quant_w1(1, 1, 2)
+        quant_w1(1, 2, 4)
+        gather_h(3, 1, 0, V)
         layer1(5)
+        fold(2, 0, V)
         gather_h(4, 0, 0, V)
-        add_z(0, 0, 256)
         gather_h(4, 1, 0, V)
-        quant_z(0, 0, 256)
-        add_z(0, 256, 512)
         layer1(6)
+        fold(3, 0, V)
         gather_h(5, 0, 0, V)
-        quant_z(0, 256, 512)
         gather_h(5, 1, 0, V)
         layer1(7)
-        gather_h(6, 0, 0, V)
-        gather_h(6, 1, 0, V)
+        fold(4, 0, 256)
+        fold(5, 0, 256)
+        weave_z(0, 0)
+        weave_z(0, 1)
+        gather_h(6, 0, 0, 256)
+        gather_h(6, 1, 0, 256)
+        fold(6, 0, 256)
         gather_h(7, 0, 0, 256)
         gather_h(7, 1, 0, 256)
+        fold(7, 0, 256)
+        weave_z(1, 0)
+        quant_z(0, 0, 512)
+        gather_h(6, 0, 256, 512)
+        gather_h(6, 1, 256, 512)
         gather_h(7, 0, 256, 512)
-        add_z(1, 0, 256)
         gather_h(7, 1, 256, 512)
-        quant_z(1, 0, 256)
-        layer2(0, 256)
         add_z(1, 256, 384)
         add_z(1, 384, 512)
+        quant_z(1, 0, 256)
+        layer2(0, 256)
         quant_z(1, 256, 384)
         layer2(256, 384)
         quant_z(1, 384, 512)

from contextlib import ExitStack

import concourse.mybir as mybir
from concourse.masks import make_identity

K, T, S, V, H, N = 512, 2048, 1024, 512, 1024, 128
P = 128
FLOPS = 2 * K * H * S + 2 * H * N * V

F32 = mybir.dt.float32
BF16 = mybir.dt.bfloat16
U32 = mybir.dt.uint32
U16 = mybir.dt.uint16
U8 = mybir.dt.uint8
FP8X4 = mybir.dt.float8_e4m3fn_x4
COPY = mybir.ActivationFunctionType.Copy
MULT = mybir.AluOpType.mult
ADD = mybir.AluOpType.add


def tile_picked_sage_none_e_kernel(tc, xT, w1, w2, gate, offs, pos1, pos2, out):
    nc = tc.nc
    with ExitStack() as ctx:
        lists = ctx.enter_context(tc.tile_pool(name="lists", bufs=1))
        sb = ctx.enter_context(tc.tile_pool(name="sb", bufs=1))
        ps = ctx.enter_context(tc.psum_pool(name="ps", bufs=1))
        ps_o = ctx.enter_context(tc.psum_pool(name="ps_o", bufs=3))
        ps_t = ctx.enter_context(tc.psum_pool(name="ps_t", bufs=2))
        ps_b = ctx.enter_context(tc.psum_pool(name="ps_b", bufs=2))

        offs_t = lists.tile([P, S // 16], U16, name="offs_t")
        pos1_t = lists.tile([P, V // 16], U16, name="pos1_t")
        pos2_t = lists.tile([P, V // 16], U16, name="pos2_t")

        warm = sb.tile([P, 1], F32, name="warm")
        warm_out = sb.tile([P, 1], F32, name="warm_out")
        nc.gpsimd.memset(warm[:], 0.0)
        nc.scalar.activation(warm_out[:], warm[:], COPY)
        ident32 = sb.tile([P, P], F32, name="ident32")
        ident16 = sb.tile([P, P], BF16, name="ident16")
        make_identity(nc, ident32[:])
        make_identity(nc, ident16[:])

        x_view = xT.rearrange("(p j) t -> p j t", j=4)
        x_raw = []
        for u, c0, c1 in ((0, 0, 1024), (0, 1024, 1536), (0, 1536, 2048), (1, 0, 1024), (1, 1024, 1536), (1, 1536, 1792), (1, 1792, 2048)):
            raw = sb.tile([P, 2, c1 - c0], F32, name="x_raw_%d_%d" % (u, c0))
            nc.sync.dma_start(raw[:], x_view[:, 2 * u : 2 * u + 2, c0:c1])
            x_raw.append((u, c0, raw))
            if len(x_raw) == 1:
                nc.sync.dma_start(offs_t[:], offs)
        w1_view = w1.rearrange("(p j) i -> p j i", j=4)
        w1_raw = []

        def load_w1(piece):
            raw = sb.tile([P, 4, 256], F32, name="w1_raw_%d" % piece)
            nc.sync.dma_start(raw[:], w1_view[:, :, 256 * piece : 256 * piece + 256])
            w1_raw.append(raw)

        load_w1(0)
        load_w1(1)
        w2_raw = sb.tile([P, 2, 4, N], F32, name="w2_raw")
        w2_view = w2.rearrange("(g p t) n -> g p t n", g=2, t=4)
        for g in range(2):
            nc.sync.dma_start(w2_raw[:, g], w2_view[g])
        nc.sync.dma_start(pos1_t[:], pos1)
        nc.sync.dma_start(pos2_t[:], pos2)
        gates = sb.tile([P, 2, V], F32, name="gates")
        nc.sync.dma_start(gates[:], gate.rearrange("d p v -> p d v"))
        load_w1(2)
        load_w1(3)

        pairs = []
        for u in range(2):
            pt = sb.tile([P, T, 2], BF16, name="pairs_%d" % u)
            pairs.append(pt)
        picked = sb.tile([P, S, 4], BF16, name="picked", align_bytes=64)
        picked_words = picked[:].rearrange("p n q -> p (n q)").bitcast(U32).rearrange("p (n u) -> p n u", u=2)
        xc0 = sb.tile([P, 512], U32, name="xc0", align_bytes=64)
        xs = sb.tile([P, S], U8, name="xs", align_bytes=64)

        def cast_x(i, a, b, scalar):
            u, c0, raw = x_raw[i]
            dst = pairs[u][:, c0 + a : c0 + b, :]
            src = raw[:, :, a:b].rearrange("p e t -> p t e")
            if scalar:
                nc.scalar.activation(dst, src, COPY)
            else:
                nc.vector.tensor_copy(dst, src)

        def gather_x(u, n0, n1):
            window = pairs[u][:].rearrange("p t e -> p (t e)").bitcast(U32)
            nc.vector.tensor_copy(picked_words[:, n0:n1, u], window.indirect(offs_t[:, n0 // 16 : n1 // 16]))

        def quant_x(n0, n1):
            nc.vector.quantize_mx(
                out=xc[n0 // 512][:].bitcast(FP8X4),
                scales=xs[:, n0:n1],
                in_=picked[:, n0:n1, :].rearrange("p n q -> p (n q)"),
            )

        w1b, w1c, w1s = [], [], []
        for g in range(2):
            b = [None, None]
            b[0] = sb.tile([P, 1, P, 4], BF16, name="w1b_%d_0" % g, align_bytes=64)
            b[1] = sb.tile([P, 3, P, 4], BF16, name="w1b_%d_1" % g, align_bytes=64)
            c = sb.tile([P, 4 * P], U32, name="w1c_%d" % g, align_bytes=64)
            s = sb.tile([P, 4 * P], U8, name="w1s_%d" % g, align_bytes=64)
            w1b.append(b)
            w1c.append(c)
            w1s.append(s)
        xc1 = sb.tile([P, 512], U32, name="xc1", tag="w1b_0_0", align_bytes=64)
        xc = (xc0, xc1)

        def cast_w1(piece, rest):
            g, half = divmod(piece, 2)
            t0, t1 = ((0, 1), (1, 4))[rest]
            dst = w1b[g][rest][:, :, 64 * half : 64 * half + 64, :].rearrange("p t m j -> p m t j")
            src = w1_raw[piece][:].rearrange("p j (m t) -> p m t j", t=4)[:, :, t0:t1, :]
            nc.scalar.activation(dst, src, COPY)

        def quant_w1(g, t0, t1):
            nc.vector.quantize_mx(
                out=w1c[g][:, P * t0 : P * t1].bitcast(FP8X4),
                scales=w1s[g][:, P * t0 : P * t1],
                in_=w1b[g][min(t0, 1)][:, max(t0 - 1, 0) : max(t1 - 1, 1)].rearrange("p t m j -> p (t m j)"),
            )

        w2b = sb.tile([P, 2, N, 4], BF16, name="w2b", tag="w1b_0_1", align_bytes=64)
        w2c = sb.tile([P, 2 * N], U32, name="w2c", align_bytes=64)
        w2s = sb.tile([P, 2 * N], U8, name="w2s", align_bytes=64)

        h = []
        for b in range(8):
            ht = sb.tile([P, S], F32, name="h_%d" % b)
            h.append(ht)
        t01, z, zc, zs = [], [], [], []
        for g in range(2):
            pair = []
            for d in range(2):
                if g:
                    tt = sb.tile([P, 4, V], F32, name="term_%d" % d)
                    pair.append([tt[:, t] for t in range(4)] + [tt])
                else:
                    blocks = []
                    for t in range(4):
                        tag = "w1b_1_%d" % d if t == 3 else "term_%d_%d" % (t, d)
                        tt = sb.tile([P, V], F32, name="term_%d_%d" % (t, d), tag=tag, align_bytes=64)
                        blocks.append(tt)
                    pair.append(blocks)
            t01.append(pair)
            zt = sb.tile([P, V, 4], BF16, name="z_%d" % g, align_bytes=64)
            zct = sb.tile([P, V], U32, name="zc_%d" % g, align_bytes=64)
            zst = sb.tile([P, V], U8, name="zs_%d" % g, align_bytes=64)
            z.append(zt)
            zc.append(zct)
            zs.append(zst)
        out_t = sb.tile([P, V], F32, name="out_t")

        def layer1(b):
            g, t = divmod(b, 4)
            for half in range(2):
                n = slice(512 * half, 512 * half + 512)
                acc = (ps_o if half else ps).tile([P, 512], F32, name="acc_%d" % half)
                nc.tensor.matmul_mx(
                    out=acc[:],
                    lhsT=w1c[g][:, P * t : P * t + P].bitcast(FP8X4),
                    lhsT_scale=w1s[g][:, P * t : P * t + P],
                    rhs=xc[half][:].bitcast(FP8X4),
                    rhs_scale=xs[:, n],
                    start=True,
                    stop=True,
                )
                nc.scalar.activation(h[b][:, n], acc[:], COPY)

        pos = (pos1_t, pos2_t)

        def gather_h(b, d, v0, v1):
            g, t = divmod(b, 4)
            nc.vector.tensor_tensor(
                t01[g][d][t][:, v0:v1],
                h[b][:].indirect(pos[d][:, v0 // 16 : v1 // 16]),
                gates[:, d, v0:v1],
                MULT,
            )

        def add_z(g, v0, v1):
            dst = z[g][:, v0:v1, :].rearrange("p (c i) t -> p c t i", i=4)
            a = t01[g][0][4][:, :, v0:v1].rearrange("p t (c i) -> p c t i", i=4)
            b = t01[g][1][4][:, :, v0:v1].rearrange("p t (c i) -> p c t i", i=4)
            nc.vector.tensor_tensor(dst, a, b, ADD)

        back = {}

        def fold(b, v0, v1):
            g, t = divmod(b, 4)
            sum_t = ps_t.tile([P, v1 - v0], F32, name="sum_t")
            for v in range(v0, v1, P):
                for d in range(2):
                    nc.tensor.matmul(
                        out=sum_t[:, v - v0 : v - v0 + P],
                        lhsT=t01[g][d][t][:, v : v + P],
                        rhs=ident32[:],
                        start=d == 0,
                        stop=d == 1,
                        is_transpose=True,
                    )
            z_t = sb.tile([P, v1 - v0], BF16, name="z_t_%d" % b)
            nc.scalar.activation(z_t[:], sum_t[:], COPY)
            for v in range(v0, v1, P):
                key = (g, v // 256)
                if key not in back:
                    back[key] = ps_b.tile([P, 4, 256], BF16, name="back")
                nc.tensor.transpose(back[key][:, t, v % 256 : v % 256 + P], z_t[:, v - v0 : v - v0 + P], ident16[:])

        def weave_z(g, half):
            nc.scalar.copy(z[g][:, 256 * half : 256 * half + 256, :], back[g, half][:].rearrange("p t v -> p v t"))

        def quant_z(g, v0, v1):
            nc.vector.quantize_mx(
                out=zc[g][:, v0:v1].bitcast(FP8X4),
                scales=zs[g][:, v0:v1],
                in_=z[g][:, v0:v1, :].rearrange("p v t -> p (v t)"),
            )

        def layer2(v0, v1):
            acc = ps_o.tile([P, v1 - v0], F32, name="acc_1")
            for g in range(2):
                nc.tensor.matmul_mx(
                    out=acc[:],
                    lhsT=w2c[:, N * g : N * g + N].bitcast(FP8X4),
                    lhsT_scale=w2s[:, N * g : N * g + N],
                    rhs=zc[g][:, v0:v1].bitcast(FP8X4),
                    rhs_scale=zs[g][:, v0:v1],
                    start=g == 0,
                    stop=g == 1,
                )
            nc.scalar.activation(out_t[:, v0:v1], acc[:], COPY)
            nc.sync.dma_start(out[:, v0:v1], out_t[:, v0:v1])

        cast_x(0, 0, 512, False)
        cast_x(0, 512, 1024, True)
        cast_x(1, 0, 512, False)
        cast_x(2, 0, 352, False)
        cast_x(2, 352, 512, True)
        gather_x(0, 0, 1024)
        cast_x(3, 0, 704, True)
        cast_x(3, 704, 1024, False)
        cast_x(4, 0, 512, False)
        cast_x(5, 0, 256, True)
        cast_x(6, 0, 256, False)
        gather_x(1, 0, 512)
        gather_x(1, 512, 1024)
        cast_w1(0, 0)
        cast_w1(0, 1)
        cast_w1(1, 0)
        cast_w1(1, 1)
        quant_x(0, 512)
        quant_w1(0, 0, 1)
        quant_x(512, 1024)
        layer1(0)
        quant_w1(0, 1, 2)
        quant_w1(0, 2, 4)
        layer1(1)
        nc.vector.tensor_copy(w2b[:], w2_raw[:].rearrange("p g t n -> p g n t"))
        layer1(2)
        layer1(3)
        cast_w1(2, 0)
        cast_w1(3, 0)
        cast_w1(2, 1)
        cast_w1(3, 1)
        gather_h(0, 0, 0, V)
        gather_h(0, 1, 0, V)
        nc.vector.quantize_mx(
            out=w2c[:].bitcast(FP8X4), scales=w2s[:], in_=w2b[:].rearrange("p g n t -> p (g n t)")
        )
        gather_h(1, 0, 0, V)
        gather_h(1, 1, 0, V)
        fold(0, 0, V)
        gather_h(2, 0, 0, V)
        gather_h(2, 1, 0, V)
        quant_w1(1, 0, 1)
        layer1(4)
        fold(1, 0, V)
        gather_h(3, 0, 0, V)
        quant_w1(1, 1, 2)
        quant_w1(1, 2, 4)
        gather_h(3, 1, 0, V)
        layer1(5)
        fold(2, 0, V)
        gather_h(4, 0, 0, V)
        gather_h(4, 1, 0, V)
        layer1(6)
        fold(3, 0, V)
        gather_h(5, 0, 0, V)
        gather_h(5, 1, 0, V)
        layer1(7)
        fold(4, 0, 256)
        fold(5, 0, 256)
        weave_z(0, 0)
        weave_z(0, 1)
        gather_h(6, 0, 0, 256)
        gather_h(6, 1, 0, 256)
        fold(6, 0, 256)
        gather_h(7, 0, 0, 256)
        gather_h(7, 1, 0, 256)
        fold(7, 0, 256)
        weave_z(1, 0)
        quant_z(0, 0, 512)
        gather_h(6, 0, 256, 512)
        gather_h(6, 1, 256, 512)
        gather_h(7, 0, 256, 512)
        gather_h(7, 1, 256, 512)
        add_z(1, 256, 384)
        add_z(1, 384, 512)
        quant_z(1, 0, 256)
        layer2(0, 256)
        quant_z(1, 256, 384)
        layer2(256, 384)
        quant_z(1, 384, 512)
        layer2(384, 512)
